import numpy as np, ml_dtypes
CORES = [17,57,65,89,97,121]
N = 6
import mx_ref
NC, G = 128, 4
C = np.float32(0.019)
BF = ml_dtypes.bfloat16
def cut(t, i, w=512):
    return t[:, w * i:w * i + w]
def tile(rs):
    return np.stack(rs, axis=2).reshape(128, -1).astype(BF)
def layer(w, X):
    out = []
    for i in range(G):
        for t in range(len(X)):
            p = mx_ref.matmul(mx_ref.quantize(cut(w, len(X) * i + t)), X[t])
            z = p if t == 0 else z + p
        out.append(z)
    return out
def act(Z):
    return [np.maximum(z, 0) * C for z in Z]
def pick(b):
    s = np.zeros((128, 128, 4), np.float32)
    s[np.arange(128), np.arange(128), b] = 1.0
    return mx_ref.quantize(s.reshape(128, 512).astype(BF))
def setup_inputs(rng):
    def f(*shape):
        return mx_ref.flush((rng.standard_normal(shape, dtype=np.float32) * np.exp2(rng.integers(-2, 3, shape[:-1] + (1,)))).astype(BF))
    return {"a": f(N, 128, G * 512), "b": f(N, 128, N * 4 * NC)}
def setup_inputs_blocks(rng):
    d = setup_inputs(rng)
    for k in ("a", "b"): d[k] = mx_ref.spread(d[k], rng, 4)
    return d
def setup_inputs_wide(rng):
    d = setup_inputs(rng)
    for k in ("a", "b"): d[k] = mx_ref.flush((d[k].astype(np.float32) * np.exp2(rng.integers(-8, 9, (N, 1, 1))).astype(np.float32)).astype(BF))
    return d
def reference(a, b):
    S = [pick(t) for t in range(4)]
    y = np.zeros((N, 128, NC, 4), np.float32)
    for c in range(N):
        for k in range(1, N + 1):
            r = (c + k) % N
            R = act(layer(a[r], [mx_ref.quantize(cut(b[r], c, 4 * NC))]))
            if k > 1: R = [R[t] + mx_ref.matmul(S[t], q) for t in range(4)]
            if k < N: q = mx_ref.quantize(tile(R))
        y[c] = np.stack(R, axis=2)
    return {"y": y.reshape(N, 128, 4 * NC)}

@@ -1,0 +1,192 @@
+from concourse.mybir import dt, AluOpType, ActivationFunctionType
+
+N = 6
+G = 4
+NC = 128
+W = 4 * NC
+BANK = 512
+FACTOR = 0.019
+
+SCRATCH = {
+    "abf": ("sbuf", [128, G * W], "bfloat16"),
+    "bbf": ("sbuf", [128, N * W], "bfloat16"),
+    "eb": ("sbuf", [128, W + 8], "bfloat16"),
+    "aq": ("sbuf", [128, G * NC], "float8_e4m3fn_x4"),
+    "aqs": ("sbuf", [128, G * NC], "uint8"),
+    "bq": ("sbuf", [128, N * NC], "float8_e4m3fn_x4"),
+    "bqs": ("sbuf", [128, N * NC], "uint8"),
+    "sq": ("sbuf", [128, G * NC], "float8_e4m3fn_x4"),
+    "sqs": ("sbuf", [128, G * NC], "uint8"),
+    "tl": ("sbuf", [128, (N - 1) * W], "bfloat16"),
+    "rb": ("sbuf", [128, (N - 1) * W], "float32"),
+    "oq": ("sbuf", [128, (N - 1) * NC], "float8_e4m3fn_x4"),
+    "oqs": ("sbuf", [128, (N - 1) * NC], "uint8"),
+    "iq": ("sbuf", [128, (N - 1) * NC], "float8_e4m3fn_x4"),
+    "iqs": ("sbuf", [128, (N - 1) * NC], "uint8"),
+    "yt": ("sbuf", [128, W], "float32"),
+    "ps": ("psum", [128, 8 * BANK], "float32"),
+}
+
+SEMAPHORES = (
+    ["lb1", "lb2", "lbg", "la0", "la1", "ones", "sel", "qs", "sent1", "sent", "st"]
+    + ["qa%d" % i for i in range(G)]
+    + ["qb%d" % k for k in range(1, N + 1)]
+    + ["p1_%d" % i for i in range(G)]
+    + ["p%d" % k for k in range(2, N + 1)]
+    + ["e%d" % k for k in range(1, N + 1)]
+    + ["d%d_%d" % (k, b) for k in range(2, N + 1) for b in range(G)]
+    + ["t%d" % k for k in range(2, N + 1)]
+    + ["q%d" % k for k in range(1, N)]
+    + ["arr%d" % k for k in range(1, N)]
+)
+
+
+def _n(mask):
+    return bin(mask).count("1")
+
+
+def _helpers(T, topo, src, dst):
+    total = topo.CHIPS * topo.CORES_PER_CHIP
+    return [c for c in range(total)
+            if topo.chip(c) == topo.chip(src) and topo.die(c) == topo.die(src)
+            and T.rank_of(c) is None and topo.may_write(c, dst)][:2]
+
+
+def _piece(T, name, k, codes):
+    v = T[name][:, NC * (k - 1):NC * k]
+    return v.bitcast(dt.uint8) if codes else v
+
+
+def _helper_program(g, core, T, topo, src, dst, codes):
+    rid, pid, se = topo.addr(dst)
+    out_mask = topo.mask(core, dst)
+    name = "iq" if codes else "iqs"
+    for k in range(1, N):
+        g.wait_ge(T.sem["arr%d" % k], _n(topo.mask(src, core)))
+        g.remote_dma(out_ap=_piece(T, name, k, codes), in_ap=_piece(T, name, k, codes),
+                     remote_sem=T.sem["arr%d" % k], local_sem=T.sem.sent,
+                     pid=pid, routing_id=rid, dma_engine_mask=out_mask)
+    g.wait_ge(T.sem.sent, (N - 1) * _n(out_mask))
+
+
+def rank_program(g, core, T, topo):
+    rank = T.rank_of(core)
+    cores = T.cores
+    if rank is None:
+        for i in range(N):
+            src, dst = cores[i], cores[(i + 1) % N]
+            helpers = _helpers(T, topo, src, dst)
+            if core in helpers:
+                _helper_program(g, core, T, topo, src, dst, core == helpers[0])
+        return
+
+    S = T.sem
+    v, te, sc, sy = g.vector, g.tensor, g.scalar, g.sync
+    helpers = _helpers(T, topo, core, cores[(rank + 1) % N])
+    n_arr = sum(_n(topo.mask(h, core)) for h in _helpers(T, topo, cores[(rank - 1) % N], core))
+    n_out = sum(_n(topo.mask(core, h)) for h in helpers)
+
+    def cols(i, w):
+        return slice(w * i, w * (i + 1))
+
+    def bank(j):
+        return T.ps[:, BANK * j:BANK * j + NC]
+
+    def load_b(q, place, c, tiles, sem):
+        q.dma_start(T.bbf[:, W * place:W * (place + tiles)], T.b[:, W * c:W * (c + tiles)]).then_inc(sem, 16)
+
+    load_b(sy, N - 1, (rank - 1) % N, 1, S.lb1)
+    sc.dma_start(T.abf[:, 0:2 * W], T.a[:, 0:2 * W]).then_inc(S.la0, 16)
+    sy.dma_start(T.abf[:, 2 * W:4 * W], T.a[:, 2 * W:4 * W]).then_inc(S.la1, 16)
+    load_b(sc, N - 2, (rank - 2) % N, 1, S.lb2)
+    sy.wait_ge(S.sent1, n_out)
+    runs, place = 0, 0
+    while place < N - 2:
+        c = (rank + place) % N
+        tiles = min(N - 2 - place, N - c)
+        load_b(sy, place, c, tiles, S.lbg)
+        place += tiles
+        runs += 1
+
+    g.wait_ge(S.ones, 1)
+    g.affine_select(T.eb[:, 0:W + 3], T.eb[:, 0:W + 3], [[-1, W + 3]], AluOpType.is_equal, 0.0, 3, 4).then_inc(S.sel, 1)
+    for k in range(1, N):
+        g.wait_ge(S["q%d" % k], 1)
+        for h, src_name, dst_name, codes in ((helpers[0], "oq", "iq", True), (helpers[1], "oqs", "iqs", False)):
+            rid, pid, se = topo.addr(h)
+            g.remote_dma(out_ap=_piece(T, dst_name, k, codes), in_ap=_piece(T, src_name, k, codes),
+                         remote_sem=S["arr%d" % k], local_sem=S.sent1 if k == 1 else S.sent,
+                         pid=pid, routing_id=rid, dma_engine_mask=topo.mask(core, h))
+    g.wait_ge(S.sent, (N - 2) * n_out)
+
+    def quant_b(k):
+        v.quantize_mx(T.bq[:, cols(N - k, NC)], T.bqs[:, cols(N - k, NC)], T.bbf[:, cols(N - k, W)]).then_inc(S["qb%d" % k], 1)
+
+    def quant_tile(k):
+        v.quantize_mx(T.oq[:, cols(k - 1, NC)], T.oqs[:, cols(k - 1, NC)], T.tl[:, cols(k - 1, W)]).then_inc(S["q%d" % k], 1)
+
+    v.memset(T.eb[:, 0:W + 3], 1.0).then_inc(S.ones, 1)
+    v.wait_ge(S.lb1, 16)
+    quant_b(1)
+    for i in range(G):
+        if i % 2 == 0:
+            v.wait_ge(S["la%d" % (i // 2)], 16)
+        v.quantize_mx(T.aq[:, cols(i, NC)], T.aqs[:, cols(i, NC)], T.abf[:, cols(i, W)]).then_inc(S["qa%d" % i], 1)
+    v.wait_ge(S.e1, G)
+    quant_tile(1)
+    v.wait_ge(S.lb2, 16)
+    quant_b(2)
+    v.wait_ge(S.sel, 1)
+    for b in range(G):
+        v.quantize_mx(T.sq[:, cols(b, NC)], T.sqs[:, cols(b, NC)], T.eb[:, 3 - b:W + 3 - b]).then_inc(S.qs, 1)
+    for k in range(2, N + 1):
+        v.wait_ge(S["e%d" % k], G)
+        for b in range(G):
+            v.wait_ge(S["d%d_%d" % (k, b)], 1)
+            out = T.tl[:, W * (k - 1) + b:W * k:4] if k < N else T.yt[:, b:W:4]
+            v.tensor_tensor(out, bank(G + b), T.rb[:, cols(G * (k - 2) + b, NC)], AluOpType.add).then_inc(S["t%d" % k], 1)
+        if k < N:
+            v.wait_ge(S["t%d" % k], G)
+            quant_tile(k)
+            if k == 2:
+                v.wait_ge(S.lbg, 16 * runs)
+            quant_b(k + 1)
+
+    def parts(k):
+        for i in range(G):
+            if k == 1:
+                te.wait_ge(S["qa%d" % i], 1)
+            te.matmul_mx(bank(i), T.aq[:, cols(i, NC)], T.aqs[:, cols(i, NC)],
+                         T.bq[:, cols(N - k, NC)], T.bqs[:, cols(N - k, NC)], True, True
+                         ).then_inc(S["p1_%d" % i] if k == 1 else S["p%d" % k], 1)
+
+    te.wait_ge(S.qb1, 1)
+    parts(1)
+    te.wait_ge(S.qb2, 1)
+    te.wait_ge(S.e1, G)
+    parts(2)
+    te.wait_ge(S.qs, G)
+    for k in range(2, N + 1):
+        te.wait_ge(S["arr%d" % (k - 1)], n_arr)
+        if k > 2:
+            te.wait_ge(S["t%d" % (k - 1)], G)
+        for b in range(G):
+            te.matmul_mx(bank(G + b), T.sq[:, cols(b, NC)], T.sqs[:, cols(b, NC)],
+                         T.iq[:, cols(k - 2, NC)], T.iqs[:, cols(k - 2, NC)], True, True).then_inc(S["d%d_%d" % (k, b)], 1)
+        if k < N:
+            te.wait_ge(S["qb%d" % (k + 1)], 1)
+            te.wait_ge(S["e%d" % k], G)
+            parts(k + 1)
+
+    for i in range(G):
+        sc.wait_ge(S["p1_%d" % i], 1)
+        sc.activation(T.tl[:, i:W:4], bank(i), ActivationFunctionType.Relu, scale=FACTOR).then_inc(S.e1, 1)
+    for k in range(2, N + 1):
+        sc.wait_ge(S["p%d" % k], G)
+        for i in range(G):
+            sc.activation(T.rb[:, cols(G * (k - 2) + i, NC)], bank(i), ActivationFunctionType.Relu,
+                          scale=FACTOR).then_inc(S["e%d" % k], 1)
+
+    sy.wait_ge(S["t%d" % N], G)
+    sy.dma_start(T.y[:], T.yt[:]).then_inc(S.st, 16)
+    sy.wait_ge(S.st, 16)

@@ -6,6 +6,8 @@ NC = 128
 W = 4 * NC
 BANK = 512
 FACTOR = 0.019
+LAST = G - 1
+HC = NC // 2
 
 SCRATCH = {
     "abf": ("sbuf", [128, G * W], "bfloat16"),
@@ -17,6 +19,8 @@ SCRATCH = {
     "bqs": ("sbuf", [128, N * NC], "uint8"),
     "sq": ("sbuf", [128, G * NC], "float8_e4m3fn_x4"),
     "sqs": ("sbuf", [128, G * NC], "uint8"),
+    "so": ("sbuf", [128, NC], "float8_e4m3fn_x4"),
+    "sos": ("sbuf", [128, NC], "uint8"),
     "tl": ("sbuf", [128, (N - 1) * W], "bfloat16"),
     "rb": ("sbuf", [128, (N - 1) * W], "float32"),
     "oq": ("sbuf", [128, (N - 1) * NC], "float8_e4m3fn_x4"),
@@ -28,7 +32,7 @@ SCRATCH = {
 }
 
 SEMAPHORES = (
-    ["lb1", "lb2", "lbg", "la0", "la1", "ones", "sel", "qs", "sent1", "sent", "st"]
+    ["sarr", "sl", "sr", "ssent", "qs3", "lb1", "lb2", "lbg", "la0", "la1", "ones", "sel", "qs", "sent1", "sent", "st"]
     + ["qa%d" % i for i in range(G)]
     + ["qb%d" % k for k in range(1, N + 1)]
     + ["p1_%d" % i for i in range(G)]
@@ -57,16 +61,46 @@ def _piece(T, name, k, codes):
     return v.bitcast(dt.uint8) if codes else v
 
 
-def _helper_program(g, core, T, topo, src, dst, codes):
+def _half(T, name, h, codes, own=False):
+    at = HC * h if own else NC * LAST + HC * h
+    v = T[name][:, at:at + HC]
+    return v.bitcast(dt.uint8) if codes else v
+
+
+def _helper_program(g, core, T, topo, src, dst, codes, other):
     rid, pid, se = topo.addr(dst)
     out_mask = topo.mask(core, dst)
-    name = "iq" if codes else "iqs"
+    n_in = _n(topo.mask(src, core))
+    name, sname = ("iq", "sq") if codes else ("iqs", "sqs")
+    left = (N + 1) * _n(out_mask)
+    if codes:
+        v = g.vector
+        v.memset(T.eb[:, 0:W], 1.0).then_inc(T.sem.ones, 1)
+        g.wait_ge(T.sem.ones, 1)
+        g.affine_select(T.eb[:, 0:W], T.eb[:, 0:W], [[-1, W]], AluOpType.is_equal, 0.0, LAST, 4).then_inc(T.sem.sel, 1)
+        v.wait_ge(T.sem.sel, 1)
+        v.quantize_mx(T.so[:], T.sos[:], T.eb[:, 0:W]).then_inc(T.sem.qs3, 1)
+        g.wait_ge(T.sem.qs3, 1)
+        g.remote_dma(out_ap=_half(T, "sq", 0, True), in_ap=_half(T, "so", 0, True, True),
+                     remote_sem=T.sem.sarr, local_sem=T.sem.sent, pid=pid, routing_id=rid, dma_engine_mask=out_mask)
+        orid, opid, ose = topo.addr(other)
+        g.remote_dma(out_ap=_half(T, "sqs", 0, False), in_ap=_half(T, "sos", 0, False, True),
+                     remote_sem=T.sem.sl, local_sem=T.sem.sent, pid=opid, routing_id=orid,
+                     dma_engine_mask=topo.mask(core, other))
+        left += _n(topo.mask(core, other))
+    else:
+        g.wait_ge(T.sem.sl, _n(topo.mask(other, core)))
+        g.remote_dma(out_ap=_half(T, "sqs", 0, False), in_ap=_half(T, "sqs", 0, False),
+                     remote_sem=T.sem.sarr, local_sem=T.sem.sent, pid=pid, routing_id=rid, dma_engine_mask=out_mask)
+    g.wait_ge(T.sem.sr, n_in)
+    g.remote_dma(out_ap=_half(T, sname, 1, codes), in_ap=_half(T, sname, 1, codes),
+                 remote_sem=T.sem.sarr, local_sem=T.sem.sent, pid=pid, routing_id=rid, dma_engine_mask=out_mask)
     for k in range(1, N):
-        g.wait_ge(T.sem["arr%d" % k], _n(topo.mask(src, core)))
+        g.wait_ge(T.sem["arr%d" % k], n_in)
         g.remote_dma(out_ap=_piece(T, name, k, codes), in_ap=_piece(T, name, k, codes),
                      remote_sem=T.sem["arr%d" % k], local_sem=T.sem.sent,
                      pid=pid, routing_id=rid, dma_engine_mask=out_mask)
-    g.wait_ge(T.sem.sent, (N - 1) * _n(out_mask))
+    g.wait_ge(T.sem.sent, left)
 
 
 def rank_program(g, core, T, topo):
@@ -77,7 +111,8 @@ def rank_program(g, core, T, topo):
             src, dst = cores[i], cores[(i + 1) % N]
             helpers = _helpers(T, topo, src, dst)
             if core in helpers:
-                _helper_program(g, core, T, topo, src, dst, core == helpers[0])
+                first = core == helpers[0]
+                _helper_program(g, core, T, topo, src, dst, first, helpers[1 if first else 0])
         return
 
     S = T.sem
@@ -98,7 +133,8 @@ def rank_program(g, core, T, topo):
     load_b(sy, N - 1, (rank - 1) % N, 1, S.lb1)
     sc.dma_start(T.abf[:, 0:2 * W], T.a[:, 0:2 * W]).then_inc(S.la0, 16)
     sy.dma_start(T.abf[:, 2 * W:4 * W], T.a[:, 2 * W:4 * W]).then_inc(S.la1, 16)
-    load_b(sc, N - 2, (rank - 2) % N, 1, S.lb2)
+    sy.wait_ge(S.ssent, n_out)
+    load_b(sy, N - 2, (rank - 2) % N, 1, S.lb2)
     sy.wait_ge(S.sent1, n_out)
     runs, place = 0, 0
     while place < N - 2:
@@ -110,6 +146,11 @@ def rank_program(g, core, T, topo):
 
     g.wait_ge(S.ones, 1)
     g.affine_select(T.eb[:, 0:W + 3], T.eb[:, 0:W + 3], [[-1, W + 3]], AluOpType.is_equal, 0.0, 3, 4).then_inc(S.sel, 1)
+    g.wait_ge(S.qs3, 1)
+    for h, src_name, dst_name, codes in ((helpers[0], "so", "sq", True), (helpers[1], "sos", "sqs", False)):
+        rid, pid, se = topo.addr(h)
+        g.remote_dma(out_ap=_half(T, dst_name, 1, codes), in_ap=_half(T, src_name, 1, codes, True),
+                     remote_sem=S.sr, local_sem=S.ssent, pid=pid, routing_id=rid, dma_engine_mask=topo.mask(core, h))
     for k in range(1, N):
         g.wait_ge(S["q%d" % k], 1)
         for h, src_name, dst_name, codes in ((helpers[0], "oq", "iq", True), (helpers[1], "oqs", "iqs", False)):
@@ -126,6 +167,8 @@ def rank_program(g, core, T, topo):
         v.quantize_mx(T.oq[:, cols(k - 1, NC)], T.oqs[:, cols(k - 1, NC)], T.tl[:, cols(k - 1, W)]).then_inc(S["q%d" % k], 1)
 
     v.memset(T.eb[:, 0:W + 3], 1.0).then_inc(S.ones, 1)
+    v.wait_ge(S.sel, 1)
+    v.quantize_mx(T.so[:], T.sos[:], T.eb[:, 3 - LAST:W + 3 - LAST]).then_inc(S.qs3, 1)
     v.wait_ge(S.lb1, 16)
     quant_b(1)
     for i in range(G):
@@ -136,8 +179,7 @@ def rank_program(g, core, T, topo):
     quant_tile(1)
     v.wait_ge(S.lb2, 16)
     quant_b(2)
-    v.wait_ge(S.sel, 1)
-    for b in range(G):
+    for b in range(LAST):
         v.quantize_mx(T.sq[:, cols(b, NC)], T.sqs[:, cols(b, NC)], T.eb[:, 3 - b:W + 3 - b]).then_inc(S.qs, 1)
     for k in range(2, N + 1):
         v.wait_ge(S["e%d" % k], G)
@@ -165,7 +207,8 @@ def rank_program(g, core, T, topo):
     te.wait_ge(S.qb2, 1)
     te.wait_ge(S.e1, G)
     parts(2)
-    te.wait_ge(S.qs, G)
+    te.wait_ge(S.qs, LAST)
+    te.wait_ge(S.sarr, 2 * n_arr)
     for k in range(2, N + 1):
         te.wait_ge(S["arr%d" % (k - 1)], n_arr)
         if k > 2:

from concourse.mybir import dt, AluOpType, ActivationFunctionType

N = 6
G = 4
NC = 128
W = 4 * NC
BANK = 512
FACTOR = 0.019
LAST = G - 1
HC = NC // 2

SCRATCH = {
    "abf": ("sbuf", [128, G * W], "bfloat16"),
    "bbf": ("sbuf", [128, N * W], "bfloat16"),
    "eb": ("sbuf", [128, W + 8], "bfloat16"),
    "aq": ("sbuf", [128, G * NC], "float8_e4m3fn_x4"),
    "aqs": ("sbuf", [128, G * NC], "uint8"),
    "bq": ("sbuf", [128, N * NC], "float8_e4m3fn_x4"),
    "bqs": ("sbuf", [128, N * NC], "uint8"),
    "sq": ("sbuf", [128, G * NC], "float8_e4m3fn_x4"),
    "sqs": ("sbuf", [128, G * NC], "uint8"),
    "so": ("sbuf", [128, NC], "float8_e4m3fn_x4"),
    "sos": ("sbuf", [128, NC], "uint8"),
    "tl": ("sbuf", [128, (N - 1) * W], "bfloat16"),
    "rb": ("sbuf", [128, (N - 1) * W], "float32"),
    "oq": ("sbuf", [128, (N - 1) * NC], "float8_e4m3fn_x4"),
    "oqs": ("sbuf", [128, (N - 1) * NC], "uint8"),
    "iq": ("sbuf", [128, (N - 1) * NC], "float8_e4m3fn_x4"),
    "iqs": ("sbuf", [128, (N - 1) * NC], "uint8"),
    "yt": ("sbuf", [128, W], "float32"),
    "ps": ("psum", [128, 8 * BANK], "float32"),
}

SEMAPHORES = (
    ["sarr", "sl", "sr", "ssent", "qs3", "lb1", "lb2", "lbg", "la0", "la1", "ones", "sel", "qs", "sent1", "sent", "st"]
    + ["qa%d" % i for i in range(G)]
    + ["qb%d" % k for k in range(1, N + 1)]
    + ["p1_%d" % i for i in range(G)]
    + ["p%d" % k for k in range(2, N + 1)]
    + ["e%d" % k for k in range(1, N + 1)]
    + ["d%d_%d" % (k, b) for k in range(2, N + 1) for b in range(G)]
    + ["t%d" % k for k in range(2, N + 1)]
    + ["q%d" % k for k in range(1, N)]
    + ["arr%d" % k for k in range(1, N)]
)


def _n(mask):
    return bin(mask).count("1")


def _helpers(T, topo, src, dst):
    total = topo.CHIPS * topo.CORES_PER_CHIP
    return [c for c in range(total)
            if topo.chip(c) == topo.chip(src) and topo.die(c) == topo.die(src)
            and T.rank_of(c) is None and topo.may_write(c, dst)][:2]


def _piece(T, name, k, codes):
    v = T[name][:, NC * (k - 1):NC * k]
    return v.bitcast(dt.uint8) if codes else v


def _half(T, name, h, codes, own=False):
    at = HC * h if own else NC * LAST + HC * h
    v = T[name][:, at:at + HC]
    return v.bitcast(dt.uint8) if codes else v


def _helper_program(g, core, T, topo, src, dst, codes, other):
    rid, pid, se = topo.addr(dst)
    out_mask = topo.mask(core, dst)
    n_in = _n(topo.mask(src, core))
    name, sname = ("iq", "sq") if codes else ("iqs", "sqs")
    left = (N + 1) * _n(out_mask)
    if codes:
        v = g.vector
        v.memset(T.eb[:, 0:W], 1.0).then_inc(T.sem.ones, 1)
        g.wait_ge(T.sem.ones, 1)
        g.affine_select(T.eb[:, 0:W], T.eb[:, 0:W], [[-1, W]], AluOpType.is_equal, 0.0, LAST, 4).then_inc(T.sem.sel, 1)
        v.wait_ge(T.sem.sel, 1)
        v.quantize_mx(T.so[:], T.sos[:], T.eb[:, 0:W]).then_inc(T.sem.qs3, 1)
        g.wait_ge(T.sem.qs3, 1)
        g.remote_dma(out_ap=_half(T, "sq", 0, True), in_ap=_half(T, "so", 0, True, True),
                     remote_sem=T.sem.sarr, local_sem=T.sem.sent, pid=pid, routing_id=rid, dma_engine_mask=out_mask)
        orid, opid, ose = topo.addr(other)
        g.remote_dma(out_ap=_half(T, "sqs", 0, False), in_ap=_half(T, "sos", 0, False, True),
                     remote_sem=T.sem.sl, local_sem=T.sem.sent, pid=opid, routing_id=orid,
                     dma_engine_mask=topo.mask(core, other))
        left += _n(topo.mask(core, other))
    else:
        g.wait_ge(T.sem.sl, _n(topo.mask(other, core)))
        g.remote_dma(out_ap=_half(T, "sqs", 0, False), in_ap=_half(T, "sqs", 0, False),
                     remote_sem=T.sem.sarr, local_sem=T.sem.sent, pid=pid, routing_id=rid, dma_engine_mask=out_mask)
    g.wait_ge(T.sem.sr, n_in)
    g.remote_dma(out_ap=_half(T, sname, 1, codes), in_ap=_half(T, sname, 1, codes),
                 remote_sem=T.sem.sarr, local_sem=T.sem.sent, pid=pid, routing_id=rid, dma_engine_mask=out_mask)
    for k in range(1, N):
        g.wait_ge(T.sem["arr%d" % k], n_in)
        g.remote_dma(out_ap=_piece(T, name, k, codes), in_ap=_piece(T, name, k, codes),
                     remote_sem=T.sem["arr%d" % k], local_sem=T.sem.sent,
                     pid=pid, routing_id=rid, dma_engine_mask=out_mask)
    g.wait_ge(T.sem.sent, left)


def rank_program(g, core, T, topo):
    rank = T.rank_of(core)
    cores = T.cores
    if rank is None:
        for i in range(N):
            src, dst = cores[i], cores[(i + 1) % N]
            helpers = _helpers(T, topo, src, dst)
            if core in helpers:
                first = core == helpers[0]
                _helper_program(g, core, T, topo, src, dst, first, helpers[1 if first else 0])
        return

    S = T.sem
    v, te, sc, sy = g.vector, g.tensor, g.scalar, g.sync
    helpers = _helpers(T, topo, core, cores[(rank + 1) % N])
    n_arr = sum(_n(topo.mask(h, core)) for h in _helpers(T, topo, cores[(rank - 1) % N], core))
    n_out = sum(_n(topo.mask(core, h)) for h in helpers)

    def cols(i, w):
        return slice(w * i, w * (i + 1))

    def bank(j):
        return T.ps[:, BANK * j:BANK * j + NC]

    def load_b(q, place, c, tiles, sem):
        q.dma_start(T.bbf[:, W * place:W * (place + tiles)], T.b[:, W * c:W * (c + tiles)]).then_inc(sem, 16)

    load_b(sy, N - 1, (rank - 1) % N, 1, S.lb1)
    sc.dma_start(T.abf[:, 0:2 * W], T.a[:, 0:2 * W]).then_inc(S.la0, 16)
    sy.dma_start(T.abf[:, 2 * W:4 * W], T.a[:, 2 * W:4 * W]).then_inc(S.la1, 16)
    sy.wait_ge(S.ssent, n_out)
    load_b(sy, N - 2, (rank - 2) % N, 1, S.lb2)
    sy.wait_ge(S.sent1, n_out)
    runs, place = 0, 0
    while place < N - 2:
        c = (rank + place) % N
        tiles = min(N - 2 - place, N - c)
        load_b(sy, place, c, tiles, S.lbg)
        place += tiles
        runs += 1

    g.wait_ge(S.ones, 1)
    g.affine_select(T.eb[:, 0:W + 3], T.eb[:, 0:W + 3], [[-1, W + 3]], AluOpType.is_equal, 0.0, 3, 4).then_inc(S.sel, 1)
    g.wait_ge(S.qs3, 1)
    for h, src_name, dst_name, codes in ((helpers[0], "so", "sq", True), (helpers[1], "sos", "sqs", False)):
        rid, pid, se = topo.addr(h)
        g.remote_dma(out_ap=_half(T, dst_name, 1, codes), in_ap=_half(T, src_name, 1, codes, True),
                     remote_sem=S.sr, local_sem=S.ssent, pid=pid, routing_id=rid, dma_engine_mask=topo.mask(core, h))
    for k in range(1, N):
        g.wait_ge(S["q%d" % k], 1)
        for h, src_name, dst_name, codes in ((helpers[0], "oq", "iq", True), (helpers[1], "oqs", "iqs", False)):
            rid, pid, se = topo.addr(h)
            g.remote_dma(out_ap=_piece(T, dst_name, k, codes), in_ap=_piece(T, src_name, k, codes),
                         remote_sem=S["arr%d" % k], local_sem=S.sent1 if k == 1 else S.sent,
                         pid=pid, routing_id=rid, dma_engine_mask=topo.mask(core, h))
    g.wait_ge(S.sent, (N - 2) * n_out)

    def quant_b(k):
        v.quantize_mx(T.bq[:, cols(N - k, NC)], T.bqs[:, cols(N - k, NC)], T.bbf[:, cols(N - k, W)]).then_inc(S["qb%d" % k], 1)

    def quant_tile(k):
        v.quantize_mx(T.oq[:, cols(k - 1, NC)], T.oqs[:, cols(k - 1, NC)], T.tl[:, cols(k - 1, W)]).then_inc(S["q%d" % k], 1)

    v.memset(T.eb[:, 0:W + 3], 1.0).then_inc(S.ones, 1)
    v.wait_ge(S.sel, 1)
    v.quantize_mx(T.so[:], T.sos[:], T.eb[:, 3 - LAST:W + 3 - LAST]).then_inc(S.qs3, 1)
    v.wait_ge(S.lb1, 16)
    quant_b(1)
    for i in range(G):
        if i % 2 == 0:
            v.wait_ge(S["la%d" % (i // 2)], 16)
        v.quantize_mx(T.aq[:, cols(i, NC)], T.aqs[:, cols(i, NC)], T.abf[:, cols(i, W)]).then_inc(S["qa%d" % i], 1)
    v.wait_ge(S.e1, G)
    quant_tile(1)
    v.wait_ge(S.lb2, 16)
    quant_b(2)
    for b in range(LAST):
        v.quantize_mx(T.sq[:, cols(b, NC)], T.sqs[:, cols(b, NC)], T.eb[:, 3 - b:W + 3 - b]).then_inc(S.qs, 1)
    for k in range(2, N + 1):
        v.wait_ge(S["e%d" % k], G)
        for b in range(G):
            v.wait_ge(S["d%d_%d" % (k, b)], 1)
            out = T.tl[:, W * (k - 1) + b:W * k:4] if k < N else T.yt[:, b:W:4]
            v.tensor_tensor(out, bank(G + b), T.rb[:, cols(G * (k - 2) + b, NC)], AluOpType.add).then_inc(S["t%d" % k], 1)
        if k < N:
            v.wait_ge(S["t%d" % k], G)
            quant_tile(k)
            if k == 2:
                v.wait_ge(S.lbg, 16 * runs)
            quant_b(k + 1)

    def parts(k):
        for i in range(G):
            if k == 1:
                te.wait_ge(S["qa%d" % i], 1)
            te.matmul_mx(bank(i), T.aq[:, cols(i, NC)], T.aqs[:, cols(i, NC)],
                         T.bq[:, cols(N - k, NC)], T.bqs[:, cols(N - k, NC)], True, True
                         ).then_inc(S["p1_%d" % i] if k == 1 else S["p%d" % k], 1)

    te.wait_ge(S.qb1, 1)
    parts(1)
    te.wait_ge(S.qb2, 1)
    te.wait_ge(S.e1, G)
    parts(2)
    te.wait_ge(S.qs, LAST)
    te.wait_ge(S.sarr, 2 * n_arr)
    for k in range(2, N + 1):
        te.wait_ge(S["arr%d" % (k - 1)], n_arr)
        if k > 2:
            te.wait_ge(S["t%d" % (k - 1)], G)
        for b in range(G):
            te.matmul_mx(bank(G + b), T.sq[:, cols(b, NC)], T.sqs[:, cols(b, NC)],
                         T.iq[:, cols(k - 2, NC)], T.iqs[:, cols(k - 2, NC)], True, True).then_inc(S["d%d_%d" % (k, b)], 1)
        if k < N:
            te.wait_ge(S["qb%d" % (k + 1)], 1)
            te.wait_ge(S["e%d" % k], G)
            parts(k + 1)

    for i in range(G):
        sc.wait_ge(S["p1_%d" % i], 1)
        sc.activation(T.tl[:, i:W:4], bank(i), ActivationFunctionType.Relu, scale=FACTOR).then_inc(S.e1, 1)
    for k in range(2, N + 1):
        sc.wait_ge(S["p%d" % k], G)
        for i in range(G):
            sc.activation(T.rb[:, cols(G * (k - 2) + i, NC)], bank(i), ActivationFunctionType.Relu,
                          scale=FACTOR).then_inc(S["e%d" % k], 1)

    sy.wait_ge(S["t%d" % N], G)
    sy.dma_start(T.y[:], T.yt[:]).then_inc(S.st, 16)
    sy.wait_ge(S.st, 16)
